import numpy as np, ml_dtypes
CORES = [13,21,141,149]
N = 4
BF = ml_dtypes.bfloat16
H, P, B, T, S = 2048, 1280, 256, 3, 32
BOUND = P + B * (np.arange(T * B) // B)
def parts(rng):
    G = P + T * B
    fe = (256 * (0.6 * rng.random((N, 8, 16, G)) + 0.4 * rng.random((N, 8, 1, G)))).astype(np.int64)
    no = (256 * (0.6 * rng.random((N, 8, 16, H)) + 0.4 * rng.random((N, 8, 1, H)))).astype(np.int64)
    no = np.minimum(no + rng.integers(0, 64, (N, 8, 1, 1)), 255)
    co = rng.integers(0, BOUND, (N, 8, 16, T * B))
    pool = np.argsort(rng.random((N, 8, H)), axis=-1)[..., :256]; ix = (256 * rng.random((N, 8, P)) ** 3).astype(np.int64)
    hv = np.where(rng.random((N, 8, P)) < 0.3, rng.integers(0, H, (N, 8, P)), np.take_along_axis(pool, ix, 2))
    return fe, no, co, hv
def pack(fe, no, co, hv):
    return {"lim": np.ascontiguousarray(no.reshape(N, 128, H)).astype(np.float32).astype(BF), "feat": np.ascontiguousarray(fe.reshape(N, 128, P + T * B)).astype(np.float32).astype(BF),
            "comp": np.ascontiguousarray(co.reshape(N, 128, T * B)).astype(np.int32), "hd": np.ascontiguousarray(hv).astype(np.int32)}
def setup_inputs(rng):
    return pack(*parts(rng))
def setup_inputs_ties(rng):
    fe, no, co, hv = parts(rng)
    d = rng.permutation(np.array([1, 2, S - 1, S, S + 1, S, 1, S + 1])).reshape(1, 8, 1, 1)
    fe = 100 + d * (rng.random(fe.shape) < 0.8).astype(np.int64); no = 100 + d * (rng.random(no.shape) < 0.35).astype(np.int64)
    fe[..., 1::2] = fe[..., 0::2].copy()
    co[:, :, 8:, ::3] = co[:, :, :8, ::3].copy()
    return pack(fe, no, co, hv)
def setup_inputs_alike(rng):
    fe, no, co, hv = parts(rng)
    hv[:, ::2] = rng.choice(np.array([0, H - 1, H // 2, 37]), (N, 4, P)); hv[..., 0] = H - 1; hv[..., P - 1] = 0
    no[:, :4] = rng.integers(200, 256, (N, 4, 16, H))
    co[:, 1] = co[:, 1, :1].copy()
    co[:, 3] = np.where(rng.random((N, 16, T * B)) < 0.5, 0, BOUND - 1)
    co[:, 5] = rng.integers(BOUND - B, BOUND, (N, 16, T * B))
    co[:, 7, 2:] = np.where(rng.random((N, 14, T * B)) < 0.5, co[:, 7, :1], co[:, 7, 1:2])
    return pack(fe, no, co, hv)
def setup_inputs_ends(rng):
    fe, no, co, hv = parts(rng); M = T * B; k = np.arange(16)[:, None]
    for g in range(5): hv[:, g] = rng.permutation(H)[:P]
    no[:, :5] = 255
    o = np.argsort(rng.random((N, 16, M)), axis=1); s = rng.integers(0, P // 2, (N, 1, M))
    fe[:, 0] = 255; fe[:, 0, :, 1:P:2] = 0
    co[:, 0] = np.where(o < 2, 2 * rng.integers(0, P // 2, (N, 1, M)) + 1, 2 * ((s + o) % (P // 2)))
    fe[:, 1, :, :P] = rng.integers(200, 256, (N, 16, P)); fe[:, 1, :, P:] = 255
    lo = np.argsort(rng.random((N, 3, T, B)), axis=-1)
    lo[:, 1:] = 0; lo[:, 2, :, 1:-1] = 1 + np.argsort(rng.random((N, T, B - 1)), axis=-1)[..., :B - 2]
    w = B + rng.integers(0, P - B, (N, 3, 1, M))
    co[:, 2:5] = np.where(k == rng.integers(0, 16, (N, 3, 1, M)), lo.reshape(N, 3, 1, M), w)
    fe[:, 2:5, :, P:] = rng.integers(0, 160, (N, 3, 16, M)); fe[:, 4, :, P::B] = 255
    for g, b in ((5, 254), (6, 0)):
        fe[:, g] = b + (rng.random((N, 16, P + M)) < 0.8).astype(np.int64); no[:, g] = b + (rng.random((N, 16, H)) < 0.3).astype(np.int64)
    return pack(fe, no, co, hv)
def setup_inputs_still(rng):
    fe, no, co, hv = parts(rng); fe = np.maximum(fe, 1)
    z = rng.integers(0, 3, (N, 8, 1, 1)); z[:, 0] = 0; z[:, 1] = 1; z[:, 2] = 2
    return pack(fe, np.where(z == 0, 255, np.where(z == 1, 0, no)), co, hv)
def setup_inputs_spread(rng):
    fe, no, co, hv = parts(rng)
    fe = (np.exp2(8 * rng.random((N, 8, 1, P + T * B))) * rng.random(fe.shape)).astype(np.int64)
    no = (np.exp2(8 * rng.random((N, 8, 1, H))) * rng.random(no.shape)).astype(np.int64)
    hv = (H * rng.random((N, 8, P)) ** 4).astype(np.int64)
    return pack(fe, no, co, hv)
def check_inputs(d):
    bad = []
    for k in ("lim", "feat"):
        x = np.asarray(d[k]).astype(np.float32)
        if not np.all((x >= 0) & (x <= 255) & (x == np.floor(x))): bad.append("whole numbers of " + k)
    if np.min(d["hd"]) < 0 or np.max(d["hd"]) > H - 1: bad.append("range of hd")
    if np.min(d["comp"]) < 0 or not np.all(np.asarray(d["comp"]) < BOUND): bad.append("range of comp")
    return bad
def reference(lim, feat, comp, hd):
    fe = feat.astype(np.float32).astype(np.int16).reshape(N, 8, 16, P + T * B); no = lim.astype(np.float32).astype(np.int16).reshape(N, 8, 16, H)
    co = comp.astype(np.int64).reshape(N, 8, 16, T * B)
    h = np.zeros((N, 8, P + T * B), np.int64); h[:, :, :P] = hd
    kappa = np.zeros(N, np.int64); ranks = np.arange(N)
    for t in range(T):
        fv = fe[..., P + t * B:P + (t + 1) * B]
        ix = co[..., t * B:(t + 1) * B].reshape(N, 8, 16 * B)
        c = np.take_along_axis(h, ix, 2)
        fc = np.take_along_axis(fe, ix[:, :, None, :], 3).reshape(N, 8, 16, 16, B)
        share = np.add.reduce(np.minimum(fv[:, :, :, None, :], fc), axis=2, dtype=np.int64)
        for a in range(N):
            q = (ranks + a) % N
            x = np.take_along_axis(no[q], c[:, :, None, :], 3).reshape(N, 8, 16, 16, B)
            n = np.add.reduce(fv[:, :, :, None, :] > x, axis=2, dtype=np.int64).reshape(N, 8, 16 * B)
            c = np.where(n >= 9, ((c * c >> 5) + c + 613 * n + kappa[q][:, None, None]) & (H - 1), c)
        c = c.reshape(N, 8, 16, B)
        m = np.add.reduce(c[:, :, :, None, :] == c[:, :, None, :, :], axis=3, dtype=np.int64)
        key = 4096 * m + share
        won = np.take_along_axis(c, np.argmax(key, axis=2)[:, :, None, :], 2)[:, :, 0]
        lost = np.take_along_axis(c, np.argmin(key, axis=2)[:, :, None, :], 2)[:, :, 0]
        h[:, :, P + t * B:P + (t + 1) * B] = won
        for r in range(N):
            for g in range(8):
                e, first = np.unique(lost[r, g], return_index=True)
                old = no[r, g][:, e]
                no[r, g][:, e] = old + np.clip(fv[r, g][:, first] - old, -S, S)
        kappa = np.add.reduce(won, axis=(1, 2)) & 255
    return {"yh": h[:, :, P:].astype(np.float32), "yl": no.reshape(N, 128, H).astype(np.float32).astype(BF)}

from concourse.bass import DstId, RemoteDMATransfer
from concourse.mybir import AluOpType as A, ActivationFunctionType as AF, AxisListType

N, H, P0, B, NT = 4, 2048, 1280, 256, 3
NB, W = 4, 64
VB = (0, 1)
HV = (1, 3)
RV = ()
PIECE = 512
CY, PCY, WAKE = 1.04, 0.52, 110.0
GV, GS = 1.8, 1.56
TUNE = (1000.0, 400.0, 4000.0, 562833, 1.0)

SCRATCH = {}
POOL = {}
_FILL = {}
_BYTES = {"float32": 4, "int32": 4, "bfloat16": 2, "float16": 2, "uint16": 2}


def sb(names, shape, dtype):
    for n in names.split():
        SCRATCH[n] = ("sbuf", shape, dtype)


def al(names, width, dtype):
    unit = 32 // _BYTES[dtype]
    for n in names.split():
        p = "p_" + dtype
        POOL[n] = (p, _FILL.get(p, 0), width)
        _FILL[p] = _FILL.get(p, 0) + -(-width // unit) * unit
        SCRATCH[p] = ("sbuf", [128, _FILL[p]], dtype)


for _s in range(N):
    sb("lm%d" % _s, [128, H + B], "bfloat16")
    al("kc%d" % _s, 1, "float32")
    al("kq%d" % _s, 128, "float16")
sb("ft", [128, 2048], "bfloat16")
sb("fv3", [128, 48, 16], "bfloat16")
sb("ci", [128, 768], "int32")
sb("hdi", [128, P0], "int32")
sb("htab", [128, 2048], "float32")
sb("hl", [128, 2 * PIECE], "bfloat16")
al("xf", 768, "float16")
al("cl", 768, "uint16")
for _t in range(NT):
    sb("fa%d fb%d" % (_t, _t), [128, 8, 256], "bfloat16")
    sb("fr%d" % _t, [128, 2048], "bfloat16")
    sb("new%d" % _t, [128, B], "bfloat16")
    sb("off%d" % _t, [128, 32], "uint16")
    sb("hlb%d" % _t, [128, 4, 8], "float16")
    al("lf%d" % _t, 16, "float32")
    al("lu%d" % _t, 16, "uint16")
    for _b in range(NB):
        al("ss%d_%d" % (_t, _b), 128, "float32")
for _t in range(NT - 1):
    for _s in range(1, N):
        sb("rn%d_%d" % (_s, _t), [128, B], "bfloat16")
        sb("ro%d_%d" % (_s, _t), [128, 32], "uint16")
    sb("hn%d" % _t, [128, B], "bfloat16")
    sb("ho%d" % _t, [128, 32], "uint16")
for _b in range(NB):
    al("hx%d" % _b, 1024, "float16")
    al("cm%d xg%d mn%d mx%d" % (_b, _b, _b, _b), 1024, "bfloat16")
    al("ul%d" % _b, W, "uint16")
    al("sq%d tb%d tc%d tr%d de%d" % (_b, _b, _b, _b, _b), W, "float32")
    al("mi%d mj%d" % (_b, _b), W, "int32")
    al("cf%d" % _b, 80, "float16")
    sb("eb%d" % _b, [128, 32, 16], "bfloat16")
    al("rr%d nr%d yy%d" % (_b, _b, _b), 128, "float32")
sb("ind", [128, 16, 272], "bfloat16")
al("lbs lbm", 256, "float16")
al("dup du1 du2 dumm", 16, "float32")
al("old dif clp", B, "bfloat16")
al("ks pf p16 gf rf b16 d2048 isr0 par npar", 1, "float32")
al("ki kj pi gi ri pa", 1, "int32")
al("io km", 256, "int32")
al("iof", 160, "float32")
al("kf", 256, "float32")
al("idw r32 bwn bws bwp bwm", 160, "float16")
al("nid id32 i613 i612 pm0 pm1 sw0 sw1 ones", 128, "float16")
al("wi onb", 128, "bfloat16")
al("c256 ta maskc", W, "float16")
al("tbn", W, "float32")
al("rsa rst", 128, "float32")
al("ub", 2048, "bfloat16")
for _b in range(NB):
    SCRATCH["pb%d" % _b] = ("psum", [128, 16, 32], "float32")
for _n in ("pe", "pd0", "pd1", "pm"):
    SCRATCH[_n] = ("psum", [128, 512], "float32")

DMASEMS = ["l_comp", "l_ci2", "l_hd", "l_ft", "l_fv", "l_lim", "st_h", "st_l"] + ["f_%d" % t for t in range(NT)]
SEMAPHORES = (["qv", "qs", "qt", "qg"] + DMASEMS + ["lm_1", "lm_2", "lm_3", "bulk0", "bulk1", "ha0", "ha1", "hls"]
              + ["%s%d" % (n, t) for t in range(NT - 1) for n in ("upo", "upn", "lo", "ln")]
              + ["uq%d_%d" % (s, t) for t in range(NT - 1) for s in (1, 3)])


def helpers(T, topo, core):
    r = T.cores.index(core)
    before, after = T.cores[(r - 1) % N], T.cores[(r + 1) % N]
    cand = [c for c in topo.cores_of(core) if c not in T.cores and topo.may_write(c, before) and topo.may_write(c, after)]
    near = [c for c in cand if topo.die(c) == topo.die(core)]
    far = [c for c in cand if topo.die(c) != topo.die(core)]
    return (near[0], far[0]), (near[1], far[1])


def helper_program(g, core, T, topo):
    S = T.sem
    for rank in T.cores:
        if core not in topo.cores_of(rank):
            continue
        r = T.cores.index(rank)
        for hs, dst, slot in zip(helpers(T, topo, rank), (T.cores[(r - 1) % N], T.cores[(r + 1) % N]), (1, 3)):
            if core not in hs:
                continue
            half = hs.index(core)
            rid, pid = topo.addr(dst, core)
            mask = topo.mask(core, dst)
            ne = len(topo.engines(core, dst))
            ls = 0
            for p in range(2):
                g.wait_ge(S["ha%d" % p], len(topo.engines(rank, core)) // 2)
                c0 = half * 2 * PIECE + p * PIECE
                g.remote_dma(T["lm%d" % slot][:, c0:c0 + PIECE], T.hl[:, p * PIECE:(p + 1) * PIECE], S["lm_%d" % slot], S.hls, pid, rid, mask)
                ls += ne
            if half == 0:
                up = len(topo.engines(rank, T.cores[(r + 2) % N]))
                for t in range(NT - 1):
                    for sem, n, h in (("upo", "ro", "ho"), ("upn", "rn", "hn")):
                        g.wait_ge(S["%s%d" % (sem, t)], up)
                        g.remote_dma(T["%s%d_%d" % (n, slot, t)][:, :], T["%s%d" % (h, t)][:, :], S["uq%d_%d" % (slot, t)], S.hls, pid, rid, mask)
                        ls += ne
            g.wait_ge(S.hls, ls)


def rank_program(g, core, T, topo):
    if T.rank_of(core) is None:
        helper_program(g, core, T, topo)
        return
    r = T.rank_of(core)
    S = T.sem
    V, C, M, Y = g.vector, g.scalar, g.tensor, g.sync
    ops, hist = [], {}
    psum = {n for n in SCRATCH if SCRATCH[n][0] == "psum"}

    def X(n, lo=0, hi=None, st=1):
        if n in POOL:
            p, o, w = POOL[n]
            t = T[p]
        else:
            t = T[n]
            o, w = 0, t.shape[1]
        if hi is None:
            hi = w
        return (t[:, o + lo:o + hi:st] if st != 1 else t[:, o + lo:o + hi], n, lo, hi)

    def X3(n, a, b, lo=0, hi=None):
        w = T[n].shape[2]
        return (T[n][:, a:b, lo:w if hi is None else hi], n, a * w, b * w)

    def XI(n, a, b, i):
        w = T[n].shape[2]
        return (T[n][:, a:b, i], n, a * w, b * w)

    def HL(n, b, lo, hi):
        return (T[n][:, b, lo:hi], n, 8 * b + lo, 8 * b + hi)

    def PB(b, a, z):
        return X3("pb%d" % b, a, z)

    def IND(win, off):
        return (win[0].indirect(off[0]), win, off)

    def split(a):
        return [a[1], a[2]] if len(a) == 3 else [a]

    def size(a):
        k = 1
        for d in a[0].shape[1:]:
            k *= d
        return k

    def add(q, busy, fire, reads, writes, sem=None, cnt=0, lat=0.0, extra=()):
        i = len(ops)
        deps = set(extra)
        acc = [(x, 0) for x in reads] + [(x, 1) for x in writes]
        for (ap, n, lo, hi), w in acc:
            past = hist.get(n, ([], []))
            for (j, jw, jlo, jhi, jq) in (past[0] + past[1] if w or n in psum else past[1]):
                if n in psum and jq != q or jhi > lo and jlo < hi and (w or jw):
                    deps.add(j)
        for (ap, n, lo, hi), w in acc:
            hist.setdefault(n, ([], []))[w].append((i, w, lo, hi, q))
        ops.append({"q": q, "busy": busy, "fire": fire, "deps": deps - {i}, "sem": sem, "cnt": cnt, "lat": lat})
        return i

    def vc(n, f):
        return max(64.0, n * f) * CY

    def tt(out, a, b, op):
        if len(a) == 3:
            return add("v", 50 + vc(size(b), GV), lambda: V.tensor_tensor(out[0], a[0], b[0], op), split(a) + [b], [out])
        return add("v", vc(size(out), 1 if (a[1] in psum or b[1] in psum) else 2), lambda: V.tensor_tensor(out[0], a[0], b[0], op), [a, b], [out])

    def ts(out, a, s1, s2, o1, o2=None, fast=False):
        rd = [a] + [s for s in (s1, s2) if isinstance(s, tuple)]
        v1 = s1[0] if isinstance(s1, tuple) else s1
        v2 = s2[0] if isinstance(s2, tuple) else s2
        if o2 is None:
            fn = lambda: V.tensor_scalar(out[0], a[0], v1, None, o1)
        else:
            fn = lambda: V.tensor_scalar(out[0], a[0], v1, v2, o1, o2)
        return add("v", vc(size(out), 0.5 if fast else 1), fn, rd, [out])

    def cp(out, a):
        if len(a) == 3:
            return add("v", 50 + vc(size(out), GS), lambda: V.tensor_copy(out[0], a[0]), split(a), [out])
        if len(out) == 3:
            return add("v", 50 + vc(size(a), 3.5), lambda: V.tensor_copy(out[0], a[0]), [a, out[2]], [out[1]])
        return add("v", vc(size(out), 1), lambda: V.tensor_copy(out[0], a[0]), [a], [out])

    def ms(out, c):
        return add("v", vc(size(out), 1), lambda: V.memset(out[0], c), [], [out])

    def act(out, a, func, bias=0.0, scale=1.0, acc=None):
        cost = 65 + vc(size(out), GS) if len(a) == 3 else 60 + vc(size(out), 1)
        if acc:
            fn = lambda: C.activation(out[0], a[0], func, bias=bias, scale=scale, accum_out=acc[0])
        else:
            fn = lambda: C.activation(out[0], a[0], func, bias=bias, scale=scale)
        return add("s", cost, fn, split(a), [out] + ([acc] if acc else []))

    def mm(lst):
        rd, wr = {}, {}
        for o, l, x, s0, s1 in lst:
            rd[l[1:]], rd[x[1:]], wr[o[1:]] = l, x, o

        def fire():
            for o, l, x, s0, s1 in lst:
                ins = M.matmul(o[0], l[0], x[0], s0, s1)
            return ins
        return add("t", sum(max(64.0, size(x[2])) for x in lst) * PCY, fire, list(rd.values()), list(wr.values()))

    def dma(q, out, in_, sem, lat):
        e = {"y": Y, "s": C}[q]
        rd = [in_] if isinstance(in_, tuple) else []
        wr = [out] if isinstance(out, tuple) else []
        src, dst_ = (in_[0] if rd else in_), (out[0] if wr else out)
        return add(q, 60, lambda: e.dma_start(dst_, src), rd, wr, sem=sem, cnt=16, lat=lat)

    ha, hb = helpers(T, topo, core)
    opp = T.cores[(r + 2) % N]
    mo = topo.mask(core, opp)
    no = len(topo.engines(core, opp))

    def dst(c):
        rid, pid = topo.addr(c, core)
        return DstId(rid=rid, pnc=pid)

    def pair(hs, p):
        tr = []
        for h in range(2):
            es = topo.engines(core, hs[h])
            k = len(es) // 2
            c0 = (2 * h + p) * PIECE
            tr.append(RemoteDMATransfer(dst_ids=[dst(hs[h])], dma_engine_mask=sum(1 << e for e in es[h * k:(h + 1) * k]), remote_sem=S["ha%d" % p],
                                        srcs=[T.lm0[:, c0:c0 + PIECE]], dsts=[T.hl[:, p * PIECE:(p + 1) * PIECE]]))
        return lambda: g.remote_dma_fused(tr, local_sem=S.bulk0)

    dma("y", X("ci", 0, 256), T.comp[:, 0:256], "l_comp", 2000)
    dma("s", X("lm0", 0, H), T.lim[:, :], "l_lim", 3500)
    dma("y", X("ft"), T.feat[:, :], "l_ft", 3500)
    ms(X("hdi"), 0)
    add("y", 60, lambda: Y.dma_start(T.hdi[0:128:16, :], T.hd[:, :]), [], [X("hdi")], sem="l_hd", cnt=16, lat=2000)
    dma("y", X3("fv3", 0, 48), T.feat[:, P0:2048], "l_fv", 2300)
    dma("s", X("ci", 256, 768), T.comp[:, 256:768], "l_ci2", 2500)
    add("g", 560, lambda: g.iota(X("io")[0], [[1, 256]], 0, 0), [], [X("io")])
    add("g", 140, lambda: g.iota(X("pi")[0], [[0, 1]], 0, 1), [], [X("pi")])

    cp(X("pf"), X("pi"))
    ts(X("ri"), X("pi"), 15, None, A.bitwise_and)
    ts(X("gi"), X("pi"), 4, None, A.logical_shift_right)
    ts(X("pa"), X("pi"), 4, 1, A.logical_shift_right, A.bitwise_and)
    cp(X("iof"), X("io", 0, 160))
    cp(X("rf"), X("ri"))
    cp(X("gf"), X("gi"))
    cp(X("par"), X("pa"))
    ts(X("npar"), X("par"), -1.0, 1.0, A.mult, A.add)
    ts(X("p16"), X("pf"), 16.0, None, A.add)
    ts(X("b16"), X("gf"), 16.0, 16.0, A.mult, A.add)
    ts(X("isr0"), X("rf"), 0.0, None, A.is_equal)
    ts(X("idw"), X("iof"), X("p16"), None, A.is_equal)
    ID = X("idw", 16, 144)

    def SL(n, s):
        return X(n, s, s + 128)
    ts(X("pm0"), ID, X("npar"), None, A.mult, fast=True)
    ts(X("pm1"), ID, X("par"), None, A.mult, fast=True)
    ts(X("sw0"), SL("idw", 0), X("npar"), None, A.mult, fast=True)
    ts(X("sw1"), SL("idw", 32), X("par"), None, A.mult, fast=True)
    ts(X("r32"), X("idw"), X("isr0"), 32.0, A.mult, A.mult, fast=True)
    for n, w in (("bwn", 19616.0), ("bws", 9808.0), ("bwp", 16.0), ("bwm", -16.0)):
        ts(X(n), X("iof"), X("b16"), w, A.is_equal, A.mult)
    for n, w in (("nid", -1.0), ("id32", 32.0), ("i613", 613.0), ("i612", 612.0), ("wi", 65536.0)):
        act(X(n), ID, AF.Copy, scale=w)

    def lists(t, b):
        c0 = t * 256 + b * W
        if b == 0:
            cp(X("xf", t * 256, t * 256 + 256), X("ci", t * 256, t * 256 + 256))
        run = []
        for j in range(4):
            o = X("pm", b * W + 16 * j, b * W + 16 * j + 16)
            k = c0 // 16 + j
            me, ot = X("xf", 16 * k, 16 * k + 16), X("xf", 16 * (k ^ 1), 16 * (k ^ 1) + 16)
            run += [(o, X("pm%d" % (k & 1)), me, True, False), (o, X("sw%d" % (k & 1)), ot, False, True)]
        mm(run)
        tr, y = X("tr%d" % b), X("pm", b * W, b * W + W)
        add("v", vc(W, 1), lambda: V.transpose(tr[0], y[0]), [y], [tr])
        cp(X("cl", c0, c0 + W), tr)

    lists(0, 0)
    cp(X("htab", 0, P0), X("hdi"))
    for b in range(1, NB):
        lists(0, b)

    def fr(t, eng):
        for half, n in ((0, "fa%d" % t), (1, "fb%d" % t)):
            a = 16 * t + 8 * half
            for k in range(16):
                o, i = T[n][:, :, 16 * k:16 * k + 16], T.fv3[:, a:a + 8, :]
                q, cost, fn = {"v": ("v", vc(128, 0.5), lambda o=o, i=i: V.tensor_copy(o, i)),
                               "s": ("s", 60 + vc(128, 1), lambda o=o, i=i: C.activation(o, i, AF.Copy)),
                               "g": ("g", 170 + 256 * CY, lambda o=o, i=i: g.affine_select(o, i, [[0, 8], [0, 16]], A.is_gt, 0.0, 1, 0))}[eng[half]]
                add(q, cost, fn, [X3("fv3", a, a + 8)], [(o, n, 128 * k, 128 * k + 128)])
            if half == 0:
                dma("y", X("fr%d" % t), X3(n, 0, 8), "f_%d" % t, 3500)

    fr(0, "vs")
    ts(X("km"), X("io"), 15, None, A.bitwise_and)
    cp(X("kf"), X("km"))
    ts(X("c256"), X("kf", 0, W), 0.0, 256.0, A.mult, A.add)
    ts(X("ones"), X("iof", 0, 128), 0.0, 1.0, A.mult, A.add)
    ts(X("ta"), X("kf", 0, W), -1.0, 15.0, A.mult, A.add)
    ts(X("tbn"), X("kf", 0, W), -2.0, 15.0, A.mult, A.add)
    for t in range(NT):
        ms(X("off%d" % t), 0)

    RL = X("lm0", 0, H)
    nb = len(topo.engines(core, ha[0]))
    rid, pid = topo.addr(opp, core)
    for p in range(2):
        add("g", 1200, pair(ha, p), [RL], [], sem="bulk0", cnt=nb, lat=3000)
    add("g", 1200, lambda: g.remote_dma(T.lm2[:, 0:H], T.lm0[:, 0:H], S.lm_2, S.bulk1, pid, rid, mo), [RL], [], sem="bulk1", cnt=no, lat=6000)
    for p in range(2):
        add("g", 1200, pair(hb, p), [RL], [], sem="bulk0", cnt=nb, lat=3000)
    for s, at in ((1, 14000), (2, 16000), (3, 20000)):
        src = T.cores[(r + s) % N]
        if s == 2:
            cnt = len(topo.engines(src, core))
        else:
            cnt = sum(2 * len(topo.engines(h, core)) for h in helpers(T, topo, src)[0 if s == 1 else 1])
        add("x", 0, None, [], [X("lm%d" % s, 0, H)], sem="lm_%d" % s, cnt=cnt, lat=at)
    for t in (1, 2):
        fr(t, "gg")

    def late():
        onb = X("onb")
        ms(onb, 1.0)
        ts(X("rsa"), X("kf", 0, 128), 0.0, -2.0e9, A.is_equal, A.mult)
        ts(X("rst"), X("rsa"), 1.0e9, None, A.add)
        ts(X("maskc"), X("kf", 0, W), X("rf"), 4096.0, A.is_ge, A.mult)
        for b in range(NB):
            ts(X("cf%d" % b, 0, 8), X("iof", 0, 8), 0.0, None, A.mult)
        ts(X("d2048"), X("rf"), 2048.0, None, A.add)
        ts(X("dumm"), X("iof", 0, 16), 16.0, X("d2048"), A.mult, A.add)
        for j in range(16):
            o = X("ub", 128 * j, 128 * j + 128)
            add("g", 170 + 256 * CY, lambda o=o, j=j: g.affine_select(o[0], onb[0], [[-16, 8], [0, 16]], A.is_equal, 0.0, -j, 1), [onb], [o])

    rot = [0]

    def diff(t, b, xg, out, func, bias):
        for h in range(2):
            d = X("pd%d" % rot[0])
            rot[0] ^= 1
            a = (b % 2) * 4 + 2 * h
            n = ("fa%d" if b < 2 else "fb%d") % t
            mm([(d, ID, (T[n][:, a:a + 2, :], n, 0, 2048), True, False), (d, X("nid"), X(xg, 512 * h, 512 * h + 512), False, True)])
            act(X(out, 512 * h, 512 * h + 512), d, func, bias=bias)

    def col(n, j):
        return X(n, j, 1024, 16)

    def halves(n, c0=0):
        return [(X(n, c0 + 32 * z, c0 + 32 * z + 32), 512 * z, 512 * z + 512) for z in range(2)]

    def shares(t, b):
        mn, win = "mn%d" % b, X("ft", 0, P0 + B * t)
        o = X("pm", 256 + W * b, 320 + W * b)
        vp = b in VB
        for cl, lo, hi in halves("cl", t * 256 + b * W):
            if vp:
                tt(X(mn, lo, hi), IND(win, cl), X("fr%d" % t, 1024 * b + lo, 1024 * b + hi), A.min)
            else:
                act(X("mx%d" % b, lo, hi), IND(win, cl), AF.Copy)
        if not vp:
            diff(t, b, "mx%d" % b, mn, AF.Relu, 0.0)
        mm([(o, ID, X("ta"), True, False)] + [(o, SL("bwp" if vp else "bwm", 16 - j), col(mn, j), False, j == 15) for j in range(16)])
        ss = "ss%d_%d" % (t, b)
        act(X(ss, 0, W), o, AF.Copy)
        tt(X(ss, W, 2 * W), X("tbn"), o, A.subtract)

    def heads(t, b):
        win, cl = X("htab", 0, P0 + B * t), X("cl", t * 256 + b * W, t * 256 + b * W + W)
        if b in HV:
            cp(X("hx%d" % b), IND(win, cl))
        else:
            act(X("hx%d" % b), IND(win, cl), AF.Copy)
        mm([(PB(b, 0, 2), SL("r32", 16 - j), col("hx%d" % b, j), j == 0, j == 15) for j in range(16)])
        ts(X("ul%d" % b), PB(b, 0, 2), 1.0 / 32, None, A.mult)
        act(X("sq%d" % b), PB(b, 0, 2), AF.Square, bias=16.0, scale=1.0 / 32)

    def visit(t, b, a):
        lm, cm = X("lm%d" % a, 0, H), "cm%d" % b
        run = [(X("kq%d" % a), X("ones", 0, W))] if t else []
        if b in VB:
            for ul, lo, hi in halves("ul%d" % b):
                tt(X(cm, lo, hi), IND(lm, ul), X("fr%d" % t, 1024 * b + lo, 1024 * b + hi), A.is_lt)
            bw = "bwn"
            if not t:
                run.append((X("nid"), X("c256")))
        else:
            for ul, lo, hi in halves("ul%d" % b):
                act(X("xg%d" % b, lo, hi), IND(lm, ul), AF.Copy)
            diff(t, b, "xg%d" % b, cm, AF.Sign, -0.5)
            bw = "bws"
            run.append((X("i613" if t else "i612"), X("c256")))
        run += [(SL(bw, 16 - j), col(cm, j)) for j in range(16)]
        mm([(PB(b, 2, 4), l, x, i == 0, i == len(run) - 1) for i, (l, x) in enumerate(run)])
        ts(X("tc%d" % b), PB(b, 2, 4), 170000.0, 16777216.0, A.is_ge, A.mult)
        tt(PB(b, 4, 6), X("sq%d" % b), PB(b, 2, 4), A.add)
        tt(X("tb%d" % b), X("tc%d" % b), PB(b, 0, 2), A.add)
        tt(X("mi%d" % b), X("tb%d" % b), PB(b, 4, 6), A.min)
        ts(X("mj%d" % b), X("mi%d" % b), 5, 2047, A.arith_shift_right, A.bitwise_and)
        if a < N - 1:
            cp(X("ul%d" % b), X("mj%d" % b))
        cp(X("cf%d" % b, 8, 72), X("mj%d" % b))
        if a < N - 1:
            mm([(PB(b, 0, 2), X("id32"), X("cf%d" % b, 8, 72), True, True)])
            act(X("sq%d" % b), PB(b, 0, 2), AF.Square, bias=16.0, scale=1.0 / 32)

    def elect(t, b):
        cf, eb, pb = "cf%d" % b, "eb%d" % b, "pb%d" % b
        c, pm, de = X(cf, 8, 72), X3(pb, 10, 14, 0, 16), X("de%d" % b)
        mm([(X3(pb, 6, 10, 0, 16), ID, c, True, True), (X3(pb, 6, 10, 16, 32), ID, c, True, True)])
        for d in range(1, 9):
            tt(X3(eb, 4 * d - 4, 4 * d), c, X3(pb, 6, 10, d, d + 16), A.is_equal)
        tt(de, X(cf, 7, 71), c, A.subtract)
        run = []
        for d in range(1, 9):
            run.append((pm, X3(eb, 4 * d - 4, 4 * d)))
            if d < 8:
                run.append((X3(pb, 10, 14, d, 16), X3(eb, 4 * d - 4, 4 * d, 0, 16 - d)))
                run.append((X3(pb, 10, 14, 0, d), X3(eb, 4 * d - 4, 4 * d, 16 - d, 16)))
        mm([(o, X("wi"), x, i == 0, i == len(run) - 1) for i, (o, x) in enumerate(run)])
        ss = "ss%d_%d" % (t, b)
        kk, rr, nr, rst = X("pe", 128 * b, 128 * b + 128), X("rr%d" % b), X("nr%d" % b), X("rst")
        tt(X("pe", 128 * b, 128 * b + W), X(ss, 0, W), pm, A.add)
        tt(X("pe", 128 * b + W, 128 * b + 2 * W), X(ss, W, 2 * W), pm, A.subtract)
        add("v", vc(128, 1), lambda: V.tensor_tensor_scan(rr[0], rst[0], kk[0], 0.0, A.min, A.max), [rst, kk], [rr])
        tt(nr, rr, kk, A.not_equal)
        for h in range(2):
            n, y = X("nr%d" % b, W * h, W * h + W), X("yy%d" % b, W * h, W * h + W)
            add("v", vc(W, 1), lambda n=n, y=y: V.tensor_tensor_scan(y[0], de[0], n[0], 0.0, A.add, A.mult), [de, n], [y])
        c15, hl = X(cf, 23, 72, 16), "hlb%d" % t
        tt(HL(hl, b, 0, 4), X("yy%d" % b, 15, 64, 16), c15, A.add)
        tt(HL(hl, b, 4, 8), X("yy%d" % b, 79, 128, 16), c15, A.add)
        tt(X("lf%d" % t, 4 * b, 4 * b + 4), X("yy%d" % b, 79, 128, 16), c15, A.add)
        mm([(XI(pb, 0, 8, j), X("ub", 128 * j, 128 * j + 128), HL(hl, b, 0, 8), True, True) for j in range(16)])
        c0 = P0 + B * t + W * b
        act(X("htab", c0, c0 + W), X3(pb, 0, 4, 0, 16), AF.Copy)

    def compare(t, b):
        lf, pl = "lf%d" % t, X3("pb%d" % b, 4, 8, 0, 16)
        cp(X("lu%d" % t, 4 * b, 4 * b + 4), X(lf, 4 * b, 4 * b + 4))
        tt(X("lbm", W * b, W * b + W), X("maskc"), pl, A.add)
        act(X("lbs", W * b, W * b + W), pl, AF.Copy)
        for j in range(4 * b, 4 * b + 4):
            def o(lo, hi):
                return (T.ind[:, j, lo:hi], "ind", 272 * j + lo, 272 * j + hi)
            if j:
                ts(o(256 - 16 * j, 256), X("lbs", 0, 16 * j), X(lf, j, j + 1), 4096.0, A.is_equal, A.mult, fast=True)
            ts(o(256, 272), X("lbm", 16 * j, 16 * j + 16), X(lf, j, j + 1), 4096.0, A.is_equal, A.mult, fast=True)
            i, d = o(256 - 16 * j, 272), X("dup", j, j + 1)
            if j in RV:
                add("v", vc(16 * j + 16, 1), lambda i=i, d=d: V.tensor_reduce(d[0], i[0], AxisListType.X, A.add), [i], [d])
            else:
                act(i, i, AF.Copy, acc=d)

    def kappa(t):
        o, ks = (T.pb0[:, 0, 0:16], "pb0", 0, 32), X("ks")
        mm([(o, X("ones"), (T["hlb%d" % t][:, :, 0:4], "hlb%d" % t, 0, 32), True, True)])
        add("v", vc(16, 1), lambda: V.tensor_reduce(ks[0], o[0], AxisListType.X, A.add), [o], [ks])
        cp(X("ki"), ks)
        ts(X("kj"), X("ki"), 255, None, A.bitwise_and)
        cp(X("off%d" % t, 16, 17), X("kj"))
        ts(X("kc0"), X("kj"), 32.0, -256.0, A.mult, A.add)
        ts(X("kq0"), ID, X("kc0"), None, A.mult, fast=True)

    def scat(a, new, off):
        cp(IND(X("lm%d" % a, 0, H + B), off), new)

    def losers(t):
        lf = "lf%d" % t
        act(X("old"), IND(X("lm0", 0, H), X("lu%d" % t)), AF.Copy)
        tt(X("dif"), X("ft", P0 + B * t, P0 + B * t + B), X("old"), A.subtract)
        ts(X("clp"), X("dif"), -32.0, 32.0, A.max, A.min, fast=True)
        tt(X("new%d" % t), X("old"), X("clp"), A.add)
        tt(X("du1"), X("dup"), X("dumm"), A.min)
        tt(X("du2"), X("du1"), X(lf), A.max)
        cp(X("off%d" % t, 0, 16), X("du2"))
        scat(0, X("new%d" % t), X("off%d" % t, 0, 16))

    def send(t):
        ids = [dst(c) for c in (opp, ha[0], hb[0])]

        def call(src, bufs, sem, ls):
            tr = [RemoteDMATransfer(dst_ids=ids, dma_engine_mask=mo, remote_sem=S[sem], srcs=[T[src][:, :]], dsts=[T[n][:, :] for n in bufs])]
            return lambda: g.remote_dma_fused(tr, local_sem=S[ls])
        sent = []
        ne = len(topo.engines(opp, core))
        for src, got, h, up, ls in (("off", "ro2", "ho", "upo", "lo"), ("new", "rn2", "hn", "upn", "ln")):
            n = "%s%d" % (src, t)
            fn = call(n, ["%s_%d" % (got, t)] + ["%s%d" % (h, t)] * 2, "%s%d" % (up, t), "%s%d" % (ls, t))
            sent.append(add("g", 1500, fn, [X(n)], [], sem="%s%d" % (ls, t), cnt=no, lat=2500))
            add("x", 0, None, [], [X("%s_%d" % (got, t))], sem="%s%d" % (up, t), cnt=ne, lat=2500, extra=(sent[-1],))
        for s in (1, 3):
            h = helpers(T, topo, T.cores[(r + s) % N])[0 if s == 1 else 1][0]
            add("x", 0, None, [], [X("ro%d_%d" % (s, t)), X("rn%d_%d" % (s, t))], sem="uq%d_%d" % (s, t), cnt=2 * len(topo.engines(h, core)), lat=6000, extra=sent)

    def receive(t, s):
        ts(X("kc%d" % s), X("ro%d_%d" % (s, t), 16, 17), 32.0, -256.0, A.mult, A.add)
        ts(X("kq%d" % s), ID, X("kc%d" % s), None, A.mult, fast=True)
        scat(s, X("rn%d_%d" % (s, t)), X("ro%d_%d" % (s, t), 0, 16))

    for t in range(NT):
        for b in range(NB):
            heads(t, b)
        for a in range(N):
            if t and a:
                receive(t - 1, a)
            for b in range(NB):
                visit(t, b, a)
            if t == 0 and a == 0:
                late()
            if t == 0 and a == 1:
                for b in range(NB):
                    shares(0, b)
        for b in range(NB):
            elect(t, b)
        for b in range(NB):
            compare(t, b)
        if t == 0:
            for tn in (1, 2):
                for b in range(NB):
                    lists(tn, b)
        if t < NT - 1:
            kappa(t)
        losers(t)
        if t < NT - 1:
            send(t)
            for b in range(NB):
                shares(t + 1, b)
    add("y", 60, lambda: Y.dma_start(T.yh[:, :], T.htab[0:128:16, P0:2048]), [X("htab", P0, 2048)], [], sem="st_h", cnt=16, lat=2000)
    dma("y", T.yl[:, :], X("lm0", 0, H), "st_l", 3500)
    emit(g, T, ops)


def schedule(ops):
    n = len(ops)
    look, fit, theta, rnd, amp = TUNE
    succ = [[] for _ in range(n)]
    need = [len(o["deps"]) for o in ops]
    for i, o in enumerate(ops):
        for j in o["deps"]:
            succ[j].append(i)
    prio = [0.0] * n
    for i in range(n - 1, -1, -1):
        o = ops[i]
        m = max([prio[j] for j in succ[i]], default=-WAKE - o["lat"]) + o["lat"] + WAKE
        rnd = (rnd * 1103515245 + 12345) % 2147483648
        prio[i] = o["busy"] * (1.0 + amp * (rnd / 2147483648.0 - 0.5)) + m
    free, ready, avail, queues = {}, [0.0] * n, {}, {}
    for i in range(n):
        if need[i] == 0:
            avail.setdefault(ops[i]["q"], []).append(i)
    end = 0.0
    for _ in range(n):
        best = None
        for q, lst in avail.items():
            if lst:
                e = max(free.get(q, 0.0), min(ready[i] for i in lst))
                if best is None or e < best[0]:
                    best = (e, q)
        e, q = best
        lst = avail[q]
        now = [i for i in lst if ready[i] <= e + 1e-6]
        pick = max(now, key=lambda i: (prio[i], -i))
        if q in "vs":
            soon = [i for i in lst if e + 1e-6 < ready[i] <= e + look and prio[i] > prio[pick] + theta]
            if soon:
                p = max(soon, key=lambda i: (prio[i], -i))
                if e + ops[pick]["busy"] > ready[p] + fit:
                    ok = [i for i in now if e + ops[i]["busy"] <= ready[p] + fit]
                    pick = max(ok, key=lambda i: (prio[i], -i)) if ok else p
        lst.remove(pick)
        o = ops[pick]
        e = max(e, ready[pick])
        fin = e + o["busy"]
        if q != "x":
            free[q] = fin
        o["t0"], o["t1"] = e, fin
        queues.setdefault(q, []).append(pick)
        comp = fin + o["lat"]
        end = max(end, comp)
        for j in succ[pick]:
            ready[j] = max(ready[j], comp + WAKE)
            need[j] -= 1
            if need[j] == 0:
                avail.setdefault(ops[j]["q"], []).append(j)
    return queues, end


def emit(g, T, ops):
    queues, end = schedule(ops)
    S = T.sem
    eng = {"v": g.vector, "s": g.scalar, "t": g.tensor, "g": g, "y": g.sync}
    qsem = {"v": "qv", "s": "qs", "t": "qt", "g": "qg"}
    wanted = set()
    for o in ops:
        wanted |= o["deps"]
    total = {}
    for q, lst in queues.items():
        for i in lst:
            o = ops[i]
            if o["sem"]:
                s, c = o["sem"], o["cnt"]
            elif i in wanted:
                s, c = qsem[q], 1
            else:
                continue
            total[s] = total.get(s, 0) + c
            o["tok"] = (s, total[s])
    for o in ops:
        if o["sem"]:
            o["tok"] = (o["sem"], total[o["sem"]])
    known = {q: {} for q in queues}
    nxt = {q: 0 for q in queues}
    done = set()
    while len(done) < len(ops):
        for q, lst in queues.items():
            kn = known[q]
            while nxt[q] < len(lst):
                i = lst[nxt[q]]
                o = ops[i]
                if not o["deps"] <= done:
                    break
                if q == "x":
                    o["clk"] = {o["tok"][0]: o["tok"][1]}
                else:
                    for j in sorted(o["deps"], key=lambda j: -ops[j]["t1"]):
                        s, v = ops[j]["tok"]
                        if kn.get(s, 0) < v:
                            eng[q].wait_ge(S[s], v)
                            for s2, v2 in ops[j]["clk"].items():
                                kn[s2] = max(kn.get(s2, 0), v2)
                            kn[s] = max(kn.get(s, 0), v)
                    ins = o["fire"]()
                    o["clk"] = dict(kn)
                    if o["sem"] in DMASEMS:
                        ins.then_inc(S[o["sem"]], 16)
                    elif not o["sem"] and i in wanted:
                        ins.then_inc(S[o["tok"][0]], 1)
                    if "tok" in o:
                        o["clk"][o["tok"][0]] = max(kn.get(o["tok"][0], 0), o["tok"][1])
                done.add(i)
                nxt[q] += 1
    for s, v in total.items():
        if known["g"].get(s, 0) < v:
            g.wait_ge(S[s], v)
